import numpy as np
import ml_dtypes

BF16 = ml_dtypes.bfloat16


def bf(x):
    return np.asarray(x, np.float32).astype(BF16)


def f32(x):
    return np.asarray(x, np.float32)


def f64(x):
    return np.asarray(x).astype(np.float64)


def striped(idx):
    return np.tile(idx.reshape(-1, 16).T, (8, 1))


S, K, M, N = 512, 512, 256, 192


def setup_inputs():
    return {"base": bf(np.random.standard_normal((M, S))), "x": bf(np.random.standard_normal((K, N))), "w": bf(np.random.standard_normal((K, M)) / np.sqrt(K)), "c": f32(0.2 + 0.8 * np.random.random_sample((1, S))), "offs": striped(np.random.permutation(S)[:N])}


def reference(base, x, w, c, offs):
    idx = offs[:16].T.reshape(-1)
    z = f64(base).copy()
    z[:, idx] += f64(w).T @ f64(x)
    return z * f64(c)

@@ -1,0 +1,56 @@
+import concourse.mybir as mybir
+from concourse.masks import make_identity
+
+P = 128
+M, S = 256, 512
+K, N = 512, 192
+M_BLOCKS = M // P
+K_BLOCKS = K // P
+
+FLOPS = 2 * K * M * N
+
+BF16, F32, U16 = mybir.dt.bfloat16, mybir.dt.float32, mybir.dt.uint16
+MULT = mybir.AluOpType.mult
+
+
+def tile_scatter_matmul_kernel(tc, base, x, w, c, offs, out):
+    nc = tc.nc
+    with (
+        tc.tile_pool(name="held", bufs=1) as held,
+        tc.psum_pool(name="banks", bufs=1) as banks,
+    ):
+        offsets = held.tile([P, N // 16], U16, name="offsets")
+        nc.sync.dma_start(offsets[:], offs)
+
+        base_sb = held.tile([P, M_BLOCKS, S], BF16, name="base_sb")
+        nc.sync.dma_start(base_sb[:], base.rearrange("(b p) s -> p b s", p=P))
+
+        w_sb = held.tile([P, K_BLOCKS, M], BF16, name="w_sb")
+        nc.scalar.dma_start(w_sb[:], w.rearrange("(p j) m -> p j m", j=K_BLOCKS))
+        x_sb = held.tile([P, K_BLOCKS, N], BF16, name="x_sb")
+        nc.scalar.dma_start(x_sb[:], x.rearrange("(p j) n -> p j n", j=K_BLOCKS))
+
+        c_all = held.tile([P, S], F32, name="c_all")
+        nc.gpsimd.dma_start(c_all[:], c.rearrange("o s -> (o s)").partition_broadcast(P))
+
+        ident = held.tile([P, P], BF16, name="ident")
+        make_identity(nc, ident[:])
+
+        windows = [banks.tile([P, S], F32, name=f"window{b}") for b in range(M_BLOCKS)]
+        for b in range(M_BLOCKS):
+            nc.tensor.matmul(windows[b][:], ident[:], base_sb[:, b, :], start=True, stop=False)
+
+        for b in range(M_BLOCKS):
+            for j in range(K_BLOCKS):
+                nc.tensor.matmul(
+                    windows[b][:].indirect(offsets[:]),
+                    w_sb[:, j, b * P : (b + 1) * P],
+                    x_sb[:, j, :],
+                    start=False,
+                    stop=(j == K_BLOCKS - 1),
+                )
+        for b in range(M_BLOCKS):
+            out_sb = held.tile([P, S], F32, name=f"out_sb{b}")
+            nc.vector.tensor_tensor(out_sb[:], windows[b][:], c_all[:], MULT)
+            store_queue = nc.sync if b % 2 == 0 else nc.scalar
+            store_queue.dma_start(out[b * P : (b + 1) * P, :], out_sb[:])

@@ -12,6 +12,8 @@ FLOPS = 2 * K * M * N
 BF16, F32, U16 = mybir.dt.bfloat16, mybir.dt.float32, mybir.dt.uint16
 MULT = mybir.AluOpType.mult
 
+WARM_UPS = 4
+
 
 def tile_scatter_matmul_kernel(tc, base, x, w, c, offs, out):
     nc = tc.nc
@@ -19,6 +21,11 @@ def tile_scatter_matmul_kernel(tc, base, x, w, c, offs, out):
         tc.tile_pool(name="held", bufs=1) as held,
         tc.psum_pool(name="banks", bufs=1) as banks,
     ):
+        zeros = held.tile([P, S], BF16, name="zeros")
+        nc.vector.memset(zeros[:], 0.0)
+        ident = held.tile([P, P], BF16, name="ident")
+        make_identity(nc, ident[:])
+
         offsets = held.tile([P, N // 16], U16, name="offsets")
         nc.sync.dma_start(offsets[:], offs)
 
@@ -31,10 +38,11 @@ def tile_scatter_matmul_kernel(tc, base, x, w, c, offs, out):
         nc.scalar.dma_start(x_sb[:], x.rearrange("(p j) n -> p j n", j=K_BLOCKS))
 
         c_all = held.tile([P, S], F32, name="c_all")
-        nc.gpsimd.dma_start(c_all[:], c.rearrange("o s -> (o s)").partition_broadcast(P))
+        nc.sync.dma_start(c_all[:], c.rearrange("o s -> (o s)").partition_broadcast(P))
 
-        ident = held.tile([P, P], BF16, name="ident")
-        make_identity(nc, ident[:])
+        warm_bank = banks.tile([P, S], F32, name="warm_bank")
+        for i in range(WARM_UPS):
+            nc.tensor.matmul(warm_bank[:], zeros[:, 0:P], zeros[:], start=True, stop=True)
 
         windows = [banks.tile([P, S], F32, name=f"window{b}") for b in range(M_BLOCKS)]
         for b in range(M_BLOCKS):

@@ -25,7 +25,11 @@ def tile_scatter_matmul_kernel(tc, base, x, w, c, offs, out):
         nc.vector.memset(zeros[:], 0.0)
         ident = held.tile([P, P], BF16, name="ident")
         make_identity(nc, ident[:])
+        ones_row = held.tile([1, P], F32, name="ones_row")
+        nc.vector.memset(ones_row[:], 1.0)
 
+        c_row = held.tile([1, S], F32, name="c_row")
+        nc.sync.dma_start(c_row[:], c)
         offsets = held.tile([P, N // 16], U16, name="offsets")
         nc.sync.dma_start(offsets[:], offs)
 
@@ -37,12 +41,14 @@ def tile_scatter_matmul_kernel(tc, base, x, w, c, offs, out):
         x_sb = held.tile([P, K_BLOCKS, N], BF16, name="x_sb")
         nc.scalar.dma_start(x_sb[:], x.rearrange("(p j) n -> p j n", j=K_BLOCKS))
 
-        c_all = held.tile([P, S], F32, name="c_all")
-        nc.sync.dma_start(c_all[:], c.rearrange("o s -> (o s)").partition_broadcast(P))
-
         warm_bank = banks.tile([P, S], F32, name="warm_bank")
         for i in range(WARM_UPS):
             nc.tensor.matmul(warm_bank[:], zeros[:, 0:P], zeros[:], start=True, stop=True)
+
+        c_bank = banks.tile([P, S], F32, name="c_bank")
+        nc.tensor.matmul(c_bank[:], ones_row[:], c_row[:], start=True, stop=True)
+        c_all = held.tile([P, S], F32, name="c_all")
+        nc.vector.tensor_copy(c_all[:], c_bank[:])
 
         windows = [banks.tile([P, S], F32, name=f"window{b}") for b in range(M_BLOCKS)]
         for b in range(M_BLOCKS):

@@ -12,6 +12,7 @@ FLOPS = 2 * K * M * N
 BF16, F32, U16 = mybir.dt.bfloat16, mybir.dt.float32, mybir.dt.uint16
 MULT = mybir.AluOpType.mult
 
+C_ROW = S // P
 WARM_UPS = 4
 
 
@@ -23,13 +24,13 @@ def tile_scatter_matmul_kernel(tc, base, x, w, c, offs, out):
     ):
         zeros = held.tile([P, S], BF16, name="zeros")
         nc.vector.memset(zeros[:], 0.0)
+        ident_f32 = held.tile([P, P], F32, name="ident_f32")
+        make_identity(nc, ident_f32[:])
         ident = held.tile([P, P], BF16, name="ident")
-        make_identity(nc, ident[:])
-        ones_row = held.tile([1, P], F32, name="ones_row")
-        nc.vector.memset(ones_row[:], 1.0)
+        nc.vector.tensor_copy(ident[:], ident_f32[:])
 
-        c_row = held.tile([1, S], F32, name="c_row")
-        nc.sync.dma_start(c_row[:], c)
+        c_col = held.tile([P, C_ROW], F32, name="c_col")
+        nc.sync.dma_start(c_col[:], c.rearrange("o (p i) -> p (o i)", i=C_ROW))
         offsets = held.tile([P, N // 16], U16, name="offsets")
         nc.sync.dma_start(offsets[:], offs)
 
@@ -45,10 +46,11 @@ def tile_scatter_matmul_kernel(tc, base, x, w, c, offs, out):
         for i in range(WARM_UPS):
             nc.tensor.matmul(warm_bank[:], zeros[:, 0:P], zeros[:], start=True, stop=True)
 
-        c_bank = banks.tile([P, S], F32, name="c_bank")
-        nc.tensor.matmul(c_bank[:], ones_row[:], c_row[:], start=True, stop=True)
-        c_all = held.tile([P, S], F32, name="c_all")
-        nc.vector.tensor_copy(c_all[:], c_bank[:])
+        c_bank = banks.tile([P, C_ROW, P], F32, name="c_bank")
+        for i in range(C_ROW):
+            nc.tensor.transpose(c_bank[:, i, :], c_col[:, i : i + 1].to_broadcast([P, P]), ident_f32[:])
+        c_all = held.tile([P, P, C_ROW], F32, name="c_all")
+        nc.vector.tensor_copy(c_all[:], c_bank[:].rearrange("q i p -> q p i"))
 
         windows = [banks.tile([P, S], F32, name=f"window{b}") for b in range(M_BLOCKS)]
         for b in range(M_BLOCKS):
@@ -65,6 +67,6 @@ def tile_scatter_matmul_kernel(tc, base, x, w, c, offs, out):
                 )
         for b in range(M_BLOCKS):
             out_sb = held.tile([P, S], F32, name=f"out_sb{b}")
-            nc.vector.tensor_tensor(out_sb[:], windows[b][:], c_all[:], MULT)
+            nc.vector.tensor_tensor(out_sb[:], windows[b][:], c_all[:].rearrange("q p i -> q (p i)"), MULT)
             store_queue = nc.sync if b % 2 == 0 else nc.scalar
             store_queue.dma_start(out[b * P : (b + 1) * P, :], out_sb[:])

@@ -13,7 +13,9 @@ BF16, F32, U16 = mybir.dt.bfloat16, mybir.dt.float32, mybir.dt.uint16
 MULT = mybir.AluOpType.mult
 
 C_ROW = S // P
-WARM_UPS = 4
+J_HALF = K_BLOCKS // 2
+S_HALF = S // 2
+WARM_UPS = 2
 
 
 def tile_scatter_matmul_kernel(tc, base, x, w, c, offs, out):
@@ -31,16 +33,18 @@ def tile_scatter_matmul_kernel(tc, base, x, w, c, offs, out):
 
         c_col = held.tile([P, C_ROW], F32, name="c_col")
         nc.sync.dma_start(c_col[:], c.rearrange("o (p i) -> p (o i)", i=C_ROW))
+        base_sb = [held.tile([P, S], BF16, name=f"base_sb{b}") for b in range(M_BLOCKS)]
+        nc.sync.dma_start(base_sb[0][:], base[0:P, :])
+        nc.scalar.dma_start(base_sb[1][:], base[P : 2 * P, :])
         offsets = held.tile([P, N // 16], U16, name="offsets")
         nc.sync.dma_start(offsets[:], offs)
-
-        base_sb = held.tile([P, M_BLOCKS, S], BF16, name="base_sb")
-        nc.sync.dma_start(base_sb[:], base.rearrange("(b p) s -> p b s", p=P))
-
-        w_sb = held.tile([P, K_BLOCKS, M], BF16, name="w_sb")
-        nc.scalar.dma_start(w_sb[:], w.rearrange("(p j) m -> p j m", j=K_BLOCKS))
-        x_sb = held.tile([P, K_BLOCKS, N], BF16, name="x_sb")
-        nc.scalar.dma_start(x_sb[:], x.rearrange("(p j) n -> p j n", j=K_BLOCKS))
+        w_view = w.rearrange("(p j) m -> p j m", j=K_BLOCKS)
+        x_view = x.rearrange("(p j) n -> p j n", j=K_BLOCKS)
+        w_half = [held.tile([P, J_HALF, M], BF16, name=f"w_half{h}") for h in range(2)]
+        x_half = [held.tile([P, J_HALF, N], BF16, name=f"x_half{h}") for h in range(2)]
+        for h in range(2):
+            nc.sync.dma_start(w_half[h][:], w_view[:, h * J_HALF : (h + 1) * J_HALF, :])
+            nc.scalar.dma_start(x_half[h][:], x_view[:, h * J_HALF : (h + 1) * J_HALF, :])
 
         warm_bank = banks.tile([P, S], F32, name="warm_bank")
         for i in range(WARM_UPS):
@@ -49,24 +53,29 @@ def tile_scatter_matmul_kernel(tc, base, x, w, c, offs, out):
         c_bank = banks.tile([P, C_ROW, P], F32, name="c_bank")
         for i in range(C_ROW):
             nc.tensor.transpose(c_bank[:, i, :], c_col[:, i : i + 1].to_broadcast([P, P]), ident_f32[:])
-        c_all = held.tile([P, P, C_ROW], F32, name="c_all")
-        nc.vector.tensor_copy(c_all[:], c_bank[:].rearrange("q i p -> q p i"))
+        c_all = held.tile([P, S], F32, name="c_all")
+        nc.vector.tensor_copy(
+            c_all[:].rearrange("q (p i) -> q p i", i=C_ROW), c_bank[:].rearrange("q i p -> q p i")
+        )
 
         windows = [banks.tile([P, S], F32, name=f"window{b}") for b in range(M_BLOCKS)]
         for b in range(M_BLOCKS):
-            nc.tensor.matmul(windows[b][:], ident[:], base_sb[:, b, :], start=True, stop=False)
+            nc.tensor.matmul(windows[b][:], ident[:], base_sb[b][:], start=True, stop=False)
 
         for b in range(M_BLOCKS):
             for j in range(K_BLOCKS):
+                h, i = divmod(j, J_HALF)
                 nc.tensor.matmul(
                     windows[b][:].indirect(offsets[:]),
-                    w_sb[:, j, b * P : (b + 1) * P],
-                    x_sb[:, j, :],
+                    w_half[h][:, i, b * P : (b + 1) * P],
+                    x_half[h][:, i, :],
                     start=False,
                     stop=(j == K_BLOCKS - 1),
                 )
+
         for b in range(M_BLOCKS):
             out_sb = held.tile([P, S], F32, name=f"out_sb{b}")
-            nc.vector.tensor_tensor(out_sb[:], windows[b][:], c_all[:].rearrange("q p i -> q (p i)"), MULT)
-            store_queue = nc.sync if b % 2 == 0 else nc.scalar
-            store_queue.dma_start(out[b * P : (b + 1) * P, :], out_sb[:])
+            for h, store_queue in enumerate((nc.scalar, nc.sync)):
+                cols = slice(h * S_HALF, (h + 1) * S_HALF)
+                nc.vector.tensor_tensor(out_sb[:, cols], windows[b][:, cols], c_all[:, cols], MULT)
+                store_queue.dma_start(out[b * P : (b + 1) * P, cols], out_sb[:, cols])

@@ -35,7 +35,7 @@ def tile_scatter_matmul_kernel(tc, base, x, w, c, offs, out):
         nc.sync.dma_start(c_col[:], c.rearrange("o (p i) -> p (o i)", i=C_ROW))
         base_sb = [held.tile([P, S], BF16, name=f"base_sb{b}") for b in range(M_BLOCKS)]
         nc.sync.dma_start(base_sb[0][:], base[0:P, :])
-        nc.scalar.dma_start(base_sb[1][:], base[P : 2 * P, :])
+        nc.sync.dma_start(base_sb[1][:], base[P : 2 * P, :])
         offsets = held.tile([P, N // 16], U16, name="offsets")
         nc.sync.dma_start(offsets[:], offs)
         w_view = w.rearrange("(p j) m -> p j m", j=K_BLOCKS)
@@ -43,8 +43,8 @@ def tile_scatter_matmul_kernel(tc, base, x, w, c, offs, out):
         w_half = [held.tile([P, J_HALF, M], BF16, name=f"w_half{h}") for h in range(2)]
         x_half = [held.tile([P, J_HALF, N], BF16, name=f"x_half{h}") for h in range(2)]
         for h in range(2):
+            nc.sync.dma_start(x_half[h][:], x_view[:, h * J_HALF : (h + 1) * J_HALF, :])
             nc.sync.dma_start(w_half[h][:], w_view[:, h * J_HALF : (h + 1) * J_HALF, :])
-            nc.scalar.dma_start(x_half[h][:], x_view[:, h * J_HALF : (h + 1) * J_HALF, :])
 
         warm_bank = banks.tile([P, S], F32, name="warm_bank")
         for i in range(WARM_UPS):

@@ -75,7 +75,7 @@ def tile_scatter_matmul_kernel(tc, base, x, w, c, offs, out):
 
         for b in range(M_BLOCKS):
             out_sb = held.tile([P, S], F32, name=f"out_sb{b}")
-            for h, store_queue in enumerate((nc.scalar, nc.sync)):
+            for h in range(S // S_HALF):
                 cols = slice(h * S_HALF, (h + 1) * S_HALF)
                 nc.vector.tensor_tensor(out_sb[:, cols], windows[b][:, cols], c_all[:, cols], MULT)
-                store_queue.dma_start(out[b * P : (b + 1) * P, cols], out_sb[:, cols])
+                nc.sync.dma_start(out[b * P : (b + 1) * P, cols], out_sb[:, cols])

@@ -24,8 +24,8 @@ def tile_scatter_matmul_kernel(tc, base, x, w, c, offs, out):
         tc.tile_pool(name="held", bufs=1) as held,
         tc.psum_pool(name="banks", bufs=1) as banks,
     ):
-        zeros = held.tile([P, S], BF16, name="zeros")
-        nc.vector.memset(zeros[:], 0.0)
+        zero = held.tile([P, 1], BF16, name="zero")
+        nc.vector.memset(zero[:], 0.0)
         ident_f32 = held.tile([P, P], F32, name="ident_f32")
         make_identity(nc, ident_f32[:])
         ident = held.tile([P, P], BF16, name="ident")
@@ -48,7 +48,9 @@ def tile_scatter_matmul_kernel(tc, base, x, w, c, offs, out):
 
         warm_bank = banks.tile([P, S], F32, name="warm_bank")
         for i in range(WARM_UPS):
-            nc.tensor.matmul(warm_bank[:], zeros[:, 0:P], zeros[:], start=True, stop=True)
+            nc.tensor.matmul(
+                warm_bank[:], zero[:].to_broadcast([P, P]), zero[:].to_broadcast([P, S]), start=True, stop=True
+            )
 
         c_bank = banks.tile([P, C_ROW, P], F32, name="c_bank")
         for i in range(C_ROW):

@@ -38,13 +38,13 @@ def tile_scatter_matmul_kernel(tc, base, x, w, c, offs, out):
         nc.sync.dma_start(base_sb[1][:], base[P : 2 * P, :])
         offsets = held.tile([P, N // 16], U16, name="offsets")
         nc.sync.dma_start(offsets[:], offs)
-        w_view = w.rearrange("(p j) m -> p j m", j=K_BLOCKS)
-        x_view = x.rearrange("(p j) n -> p j n", j=K_BLOCKS)
+        w_view = w.rearrange("(h p i) m -> h p i m", h=2, i=J_HALF)
+        x_view = x.rearrange("(h p i) n -> h p i n", h=2, i=J_HALF)
         w_half = [held.tile([P, J_HALF, M], BF16, name=f"w_half{h}") for h in range(2)]
         x_half = [held.tile([P, J_HALF, N], BF16, name=f"x_half{h}") for h in range(2)]
         for h in range(2):
-            nc.sync.dma_start(x_half[h][:], x_view[:, h * J_HALF : (h + 1) * J_HALF, :])
-            nc.sync.dma_start(w_half[h][:], w_view[:, h * J_HALF : (h + 1) * J_HALF, :])
+            nc.sync.dma_start(x_half[h][:], x_view[h])
+            nc.sync.dma_start(w_half[h][:], w_view[h])
 
         warm_bank = banks.tile([P, S], F32, name="warm_bank")
         for i in range(WARM_UPS):

@@ -31,11 +31,11 @@ def tile_scatter_matmul_kernel(tc, base, x, w, c, offs, out):
         ident = held.tile([P, P], BF16, name="ident")
         nc.vector.tensor_copy(ident[:], ident_f32[:])
 
-        c_col = held.tile([P, C_ROW], F32, name="c_col")
-        nc.sync.dma_start(c_col[:], c.rearrange("o (p i) -> p (o i)", i=C_ROW))
         base_sb = [held.tile([P, S], BF16, name=f"base_sb{b}") for b in range(M_BLOCKS)]
         nc.sync.dma_start(base_sb[0][:], base[0:P, :])
         nc.sync.dma_start(base_sb[1][:], base[P : 2 * P, :])
+        c_col = held.tile([P, C_ROW], F32, name="c_col")
+        nc.sync.dma_start(c_col[:], c.rearrange("o (p i) -> p (o i)", i=C_ROW))
         offsets = held.tile([P, N // 16], U16, name="offsets")
         nc.sync.dma_start(offsets[:], offs)
         w_view = w.rearrange("(h p i) m -> h p i m", h=2, i=J_HALF)
@@ -52,6 +52,10 @@ def tile_scatter_matmul_kernel(tc, base, x, w, c, offs, out):
                 warm_bank[:], zero[:].to_broadcast([P, P]), zero[:].to_broadcast([P, S]), start=True, stop=True
             )
 
+        windows = [banks.tile([P, S], F32, name=f"window{b}") for b in range(M_BLOCKS)]
+        for b in range(M_BLOCKS):
+            nc.tensor.matmul(windows[b][:], ident[:], base_sb[b][:], start=True, stop=False)
+
         c_bank = banks.tile([P, C_ROW, P], F32, name="c_bank")
         for i in range(C_ROW):
             nc.tensor.transpose(c_bank[:, i, :], c_col[:, i : i + 1].to_broadcast([P, P]), ident_f32[:])
@@ -59,10 +63,6 @@ def tile_scatter_matmul_kernel(tc, base, x, w, c, offs, out):
         nc.vector.tensor_copy(
             c_all[:].rearrange("q (p i) -> q p i", i=C_ROW), c_bank[:].rearrange("q i p -> q p i")
         )
-
-        windows = [banks.tile([P, S], F32, name=f"window{b}") for b in range(M_BLOCKS)]
-        for b in range(M_BLOCKS):
-            nc.tensor.matmul(windows[b][:], ident[:], base_sb[b][:], start=True, stop=False)
 
         for b in range(M_BLOCKS):
             for j in range(K_BLOCKS):

@@ -15,7 +15,7 @@ MULT = mybir.AluOpType.mult
 C_ROW = S // P
 J_HALF = K_BLOCKS // 2
 S_HALF = S // 2
-WARM_UPS = 2
+WARM_UPS = 4
 
 
 def tile_scatter_matmul_kernel(tc, base, x, w, c, offs, out):

@@ -26,10 +26,11 @@ def tile_scatter_matmul_kernel(tc, base, x, w, c, offs, out):
     ):
         zero = held.tile([P, 1], BF16, name="zero")
         nc.vector.memset(zero[:], 0.0)
-        ident_f32 = held.tile([P, P], F32, name="ident_f32")
-        make_identity(nc, ident_f32[:])
         ident = held.tile([P, P], BF16, name="ident")
-        nc.vector.tensor_copy(ident[:], ident_f32[:])
+        ident_f32 = held.tile([P, P], F32, name="ident_f32")
+        for square in (ident, ident_f32):
+            nc.vector.memset(square[:], 0.0)
+            make_identity(nc, square[:], nomemset=True)
 
         base_sb = [held.tile([P, S], BF16, name=f"base_sb{b}") for b in range(M_BLOCKS)]
         nc.sync.dma_start(base_sb[0][:], base[0:P, :])

@@ -15,7 +15,7 @@ MULT = mybir.AluOpType.mult
 C_ROW = S // P
 J_HALF = K_BLOCKS // 2
 S_HALF = S // 2
-WARM_UPS = 4
+WARM_UPS = 3
 
 
 def tile_scatter_matmul_kernel(tc, base, x, w, c, offs, out):

@@ -14,6 +14,7 @@ MULT = mybir.AluOpType.mult
 
 C_ROW = S // P
 J_HALF = K_BLOCKS // 2
+REST = K_BLOCKS - 1
 S_HALF = S // 2
 WARM_UPS = 3
 
@@ -39,13 +40,17 @@ def tile_scatter_matmul_kernel(tc, base, x, w, c, offs, out):
         nc.sync.dma_start(c_col[:], c.rearrange("o (p i) -> p (o i)", i=C_ROW))
         offsets = held.tile([P, N // 16], U16, name="offsets")
         nc.sync.dma_start(offsets[:], offs)
-        w_view = w.rearrange("(h p i) m -> h p i m", h=2, i=J_HALF)
-        x_view = x.rearrange("(h p i) n -> h p i n", h=2, i=J_HALF)
-        w_half = [held.tile([P, J_HALF, M], BF16, name=f"w_half{h}") for h in range(2)]
+        x_view = x.rearrange("(p h i) n -> h p i n", h=2, i=J_HALF)
+        w_view = w.rearrange("(p j) m -> p j m", j=K_BLOCKS)
         x_half = [held.tile([P, J_HALF, N], BF16, name=f"x_half{h}") for h in range(2)]
-        for h in range(2):
-            nc.sync.dma_start(x_half[h][:], x_view[h])
-            nc.sync.dma_start(w_half[h][:], w_view[h])
+        w_first = held.tile([P, 1, M], BF16, name="w_first")
+        w_rest = held.tile([P, REST, M], BF16, name="w_rest")
+        nc.sync.dma_start(x_half[0][:], x_view[0])
+        nc.sync.dma_start(w_first[:], w_view[:, 0:1, :])
+        nc.sync.dma_start(w_rest[:], w_view[:, 1:K_BLOCKS, :])
+        nc.sync.dma_start(x_half[1][:], x_view[1])
+        w_block = [w_first[:, 0, :]] + [w_rest[:, j, :] for j in range(REST)]
+        x_block = [x_half[h][:, i, :] for h in range(2) for i in range(J_HALF)]
 
         warm_bank = banks.tile([P, S], F32, name="warm_bank")
         for i in range(WARM_UPS):
@@ -65,16 +70,16 @@ def tile_scatter_matmul_kernel(tc, base, x, w, c, offs, out):
             c_all[:].rearrange("q (p i) -> q p i", i=C_ROW), c_bank[:].rearrange("q i p -> q p i")
         )
 
-        for b in range(M_BLOCKS):
-            for j in range(K_BLOCKS):
-                h, i = divmod(j, J_HALF)
-                nc.tensor.matmul(
-                    windows[b][:].indirect(offsets[:]),
-                    w_half[h][:, i, b * P : (b + 1) * P],
-                    x_half[h][:, i, :],
-                    start=False,
-                    stop=(j == K_BLOCKS - 1),
-                )
+        first = [(b, 0) for b in range(M_BLOCKS)]
+        rest = [(b, j) for b in range(M_BLOCKS) for j in range(1, K_BLOCKS)]
+        for b, j in first + rest:
+            nc.tensor.matmul(
+                windows[b][:].indirect(offsets[:]),
+                w_block[j][:, b * P : (b + 1) * P],
+                x_block[j],
+                start=False,
+                stop=(j == K_BLOCKS - 1),
+            )
 
         for b in range(M_BLOCKS):
             out_sb = held.tile([P, S], F32, name=f"out_sb{b}")

@@ -16,7 +16,7 @@ C_ROW = S // P
 J_HALF = K_BLOCKS // 2
 REST = K_BLOCKS - 1
 S_HALF = S // 2
-WARM_UPS = 3
+WARM_UPS = 4
 
 
 def tile_scatter_matmul_kernel(tc, base, x, w, c, offs, out):

import concourse.mybir as mybir
from concourse.masks import make_identity

P = 128
M, S = 256, 512
K, N = 512, 192
M_BLOCKS = M // P
K_BLOCKS = K // P

FLOPS = 2 * K * M * N

BF16, F32, U16 = mybir.dt.bfloat16, mybir.dt.float32, mybir.dt.uint16
MULT = mybir.AluOpType.mult

C_ROW = S // P
J_HALF = K_BLOCKS // 2
REST = K_BLOCKS - 1
S_HALF = S // 2
WARM_UPS = 4


def tile_scatter_matmul_kernel(tc, base, x, w, c, offs, out):
    nc = tc.nc
    with (
        tc.tile_pool(name="held", bufs=1) as held,
        tc.psum_pool(name="banks", bufs=1) as banks,
    ):
        zero = held.tile([P, 1], BF16, name="zero")
        nc.vector.memset(zero[:], 0.0)
        ident = held.tile([P, P], BF16, name="ident")
        ident_f32 = held.tile([P, P], F32, name="ident_f32")
        for square in (ident, ident_f32):
            nc.vector.memset(square[:], 0.0)
            make_identity(nc, square[:], nomemset=True)

        base_sb = [held.tile([P, S], BF16, name=f"base_sb{b}") for b in range(M_BLOCKS)]
        nc.sync.dma_start(base_sb[0][:], base[0:P, :])
        nc.sync.dma_start(base_sb[1][:], base[P : 2 * P, :])
        c_col = held.tile([P, C_ROW], F32, name="c_col")
        nc.sync.dma_start(c_col[:], c.rearrange("o (p i) -> p (o i)", i=C_ROW))
        offsets = held.tile([P, N // 16], U16, name="offsets")
        nc.sync.dma_start(offsets[:], offs)
        x_view = x.rearrange("(p h i) n -> h p i n", h=2, i=J_HALF)
        w_view = w.rearrange("(p j) m -> p j m", j=K_BLOCKS)
        x_half = [held.tile([P, J_HALF, N], BF16, name=f"x_half{h}") for h in range(2)]
        w_first = held.tile([P, 1, M], BF16, name="w_first")
        w_rest = held.tile([P, REST, M], BF16, name="w_rest")
        nc.sync.dma_start(x_half[0][:], x_view[0])
        nc.sync.dma_start(w_first[:], w_view[:, 0:1, :])
        nc.sync.dma_start(w_rest[:], w_view[:, 1:K_BLOCKS, :])
        nc.sync.dma_start(x_half[1][:], x_view[1])
        w_block = [w_first[:, 0, :]] + [w_rest[:, j, :] for j in range(REST)]
        x_block = [x_half[h][:, i, :] for h in range(2) for i in range(J_HALF)]

        warm_bank = banks.tile([P, S], F32, name="warm_bank")
        for i in range(WARM_UPS):
            nc.tensor.matmul(
                warm_bank[:], zero[:].to_broadcast([P, P]), zero[:].to_broadcast([P, S]), start=True, stop=True
            )

        windows = [banks.tile([P, S], F32, name=f"window{b}") for b in range(M_BLOCKS)]
        for b in range(M_BLOCKS):
            nc.tensor.matmul(windows[b][:], ident[:], base_sb[b][:], start=True, stop=False)

        c_bank = banks.tile([P, C_ROW, P], F32, name="c_bank")
        for i in range(C_ROW):
            nc.tensor.transpose(c_bank[:, i, :], c_col[:, i : i + 1].to_broadcast([P, P]), ident_f32[:])
        c_all = held.tile([P, S], F32, name="c_all")
        nc.vector.tensor_copy(
            c_all[:].rearrange("q (p i) -> q p i", i=C_ROW), c_bank[:].rearrange("q i p -> q p i")
        )

        first = [(b, 0) for b in range(M_BLOCKS)]
        rest = [(b, j) for b in range(M_BLOCKS) for j in range(1, K_BLOCKS)]
        for b, j in first + rest:
            nc.tensor.matmul(
                windows[b][:].indirect(offsets[:]),
                w_block[j][:, b * P : (b + 1) * P],
                x_block[j],
                start=False,
                stop=(j == K_BLOCKS - 1),
            )

        for b in range(M_BLOCKS):
            out_sb = held.tile([P, S], F32, name=f"out_sb{b}")
            for h in range(S // S_HALF):
                cols = slice(h * S_HALF, (h + 1) * S_HALF)
                nc.vector.tensor_tensor(out_sb[:, cols], windows[b][:, cols], c_all[:, cols], MULT)
                nc.sync.dma_start(out[b * P : (b + 1) * P, cols], out_sb[:, cols])
